import numpy as np
import ml_dtypes


def mxq(x, axis, fmt="e4m3"):
    dtype, down = {"e4m3": (ml_dtypes.float8_e4m3fn, 7), "e5m2": (ml_dtypes.float8_e5m2, 14)}[fmt]
    v = np.moveaxis(np.asarray(x, np.float32).astype(ml_dtypes.bfloat16).astype(np.float64), axis, -1)
    blocks = v.reshape(v.shape[:-1] + (-1, 32))
    amax = np.abs(blocks).max(-1, keepdims=True)
    byte = np.maximum(np.where(amax > 0, np.frexp(amax)[1] - 1 + 127, 0) - down, 1)
    scale = np.exp2(byte - 127.0)
    codes = (blocks / scale).astype(np.float32).astype(dtype).astype(np.float64)
    return np.moveaxis((codes * scale).reshape(v.shape), -1, axis)


WIDE = False


def mx_kscale(k):
    if not WIDE:
        return np.ones(k)
    levels = np.array([10, -10, 5, -5, 0])
    if k % 512:
        return np.exp2(np.random.permutation(np.resize(levels, k // 32))).repeat(32)
    a = np.empty((k // 512, 16))
    for p in range(k // 512):
        a[p, :8] = np.random.permutation(np.resize(levels, 8))
        for g in range(8):
            far = levels[np.abs(levels - a[p, g]) >= 10]
            a[p, g + 8] = far[np.random.randint(len(far))]
    return np.exp2(a.ravel()).repeat(32)


def f64(x):
    return np.asarray(x).astype(np.float64)


def striped(idx):
    return np.tile(idx.reshape(-1, 16).T, (8, 1)).astype(np.uint16)


def unstriped(offs):
    return offs[:16].T.reshape(-1).astype(np.int64)


def pack_weight(w):
    k, n = w.shape
    w = f64(np.asarray(w, np.float32).astype(ml_dtypes.bfloat16)).reshape(k // 32, 32, n)
    amax = np.abs(w).max(1)
    byte = np.clip(np.where(amax > 0, np.frexp(amax)[1] - 1 + 127 - 7, 1), 1, 254)
    scaled = (w * np.exp2(127.0 - byte)[:, None, :]).reshape(k, n).astype(np.float32)
    words = np.ascontiguousarray(scaled.reshape(k // 512, 128, 4, n).transpose(0, 1, 3, 2)).astype(ml_dtypes.float8_e4m3fn).view(np.uint8)
    return words, np.ascontiguousarray(byte.astype(np.uint8).reshape(k // 512, 16, n))


def unpack_weight(words, scales):
    g, p, n, _ = words.shape
    vals = np.ascontiguousarray(words).view(ml_dtypes.float8_e4m3fn).astype(np.float64) * np.repeat(np.exp2(scales.astype(np.float64) - 127.0), 8, axis=1)[..., None]
    return vals.transpose(0, 1, 3, 2).reshape(g * 512, n)


def relu(v):
    return np.maximum(v, 0.0)


def sigmoid(v):
    return 1.0 / (1.0 + np.exp(-np.maximum(v, -700.0)))


K, T, S, D, N = 1024, 2048, 1024, 4, 256
P = 2 ** 7


def setup_inputs():
    n = np.random.standard_normal
    s = mx_kscale(K)[:, None]
    packed_xT = pack_weight(n((K, T)) * s)
    return {
        "x_words": packed_xT[0],
        "x_scales": packed_xT[1],
        "w1": (n((K, N)) / np.sqrt(K) / s).astype(np.float32),
        "lam": (np.tile(np.random.uniform(0.5, 1.5, S), (P, 1))).astype(np.float32),
        "one": (np.tile(np.random.uniform(0.8, 1.0, S), (P, 1))).astype(np.float32),
        "scl": (np.random.uniform(0.3, 1.0, (N, 1))).astype(np.float32),
        "offs": striped(np.random.permutation(T)[:S]),
    }


def reference(x_words, x_scales, w1, lam, one, scl, offs):
    xq = unpack_weight(x_words, x_scales)[:, unstriped(offs)]
    y = mxq(f64(w1), 0, "e4m3").T @ xq
    pos = relu(y - 0.3)
    pl = pos * f64(lam)[:1]
    psum = pl.reshape(len(pl), -1, D).sum(axis=2)
    ngt = relu(-1.0 * y - 0.3)
    nl = ngt * f64(lam)[:1]
    nsum = nl.reshape(len(nl), -1, D).sum(axis=2)
    sel = sigmoid(6.0 * (psum - nsum))
    kp = np.minimum(4.0 * pos, f64(one)[:1])
    kn = np.minimum(4.0 * ngt, f64(one)[:1])
    return np.abs(psum - nsum) * (np.exp(-1.0 * (psum + nsum))) + f64(scl) * (sel * (psum / (kp.reshape(len(kp), -1, D).sum(axis=2) + 0.3)) - ((-1.0 * sel + 1.0) * (nsum / (kn.reshape(len(kn), -1, D).sum(axis=2) + 0.3))))

@@ -1,0 +1,236 @@
+from contextlib import ExitStack
+
+import concourse.mybir as mybir
+from concourse.masks import make_identity
+
+K, T, S, D, N = 1024, 2048, 1024, 4, 256
+FLOPS = 2 * K * S * N
+P = 128
+PACK = 4
+PASSES = K // (P * PACK)
+HALVES = S // (P * D)
+HALF = P * D
+MB = N // P
+CUT = 0.3
+GAIN = 4.0
+FLOOR = 0.3
+
+F32 = mybir.dt.float32
+BF16 = mybir.dt.bfloat16
+I32 = mybir.dt.int32
+U32 = mybir.dt.uint32
+U16 = mybir.dt.uint16
+U8 = mybir.dt.uint8
+FP8X4 = mybir.dt.float8_e4m3fn_x4
+ALU = mybir.AluOpType
+ACT = mybir.ActivationFunctionType
+AX = mybir.AxisListType
+
+
+def tile_picked_ytiesm_dis_p_kernel(tc, x_words, x_scales, w1, lam, one, scl, offs, out):
+    nc = tc.nc
+    with ExitStack() as ctx:
+        keep = ctx.enter_context(tc.tile_pool(name="keep", bufs=1))
+        psum = ctx.enter_context(tc.psum_pool(name="psum", bufs=1))
+
+        offsets = keep.tile([P, S // 16], U16, name="offsets")
+        nc.sync.dma_start(offsets[:], offs)
+
+        scale_win = keep.tile([P, T], U8, name="scale_win", align_bytes=64)
+        nc.vector.memset(scale_win[:].bitcast(I32), 0)
+        for q in range(4):
+            nc.scalar.dma_start(
+                scale_win[32 * q : 32 * q + 4 * PASSES, :].bitcast(I32),
+                x_scales[:, 4 * q : 4 * q + 4, :].bitcast(I32),
+            )
+
+        warm = keep.tile([P, 2], F32, name="warm")
+        nc.vector.memset(warm[:, 0:1], 1.0)
+        nc.scalar.activation(warm[:, 1:2], warm[:, 0:1], ACT.Abs_reciprocal_sqrt)
+
+        word_win = [keep.tile([P, T], U32, name="word_win%d" % o, align_bytes=64) for o in range(PASSES)]
+        w_raw = [keep.tile([P, PACK, N], F32, name="w_raw%d" % o) for o in range(PASSES)]
+
+        def load_words(o):
+            nc.sync.dma_start(word_win[o][:].bitcast(I32), x_words[o].rearrange("p n t -> p (n t)").bitcast(I32))
+
+        load_words(0)
+        for o in range(PASSES):
+            nc.sync.dma_start(w_raw[o][:], w1[o * P * PACK : (o + 1) * P * PACK, :].rearrange("(p j) n -> p j n", j=PACK))
+        load_words(1)
+
+        lam_t = keep.tile([P, HALVES, D], F32, name="lam_t")
+        one_t = keep.tile([P, HALVES, D], F32, name="one_t")
+        scl_t = keep.tile([P, MB], F32, name="scl_t")
+        nc.sync.dma_start(lam_t[:], lam[0, :].rearrange("(b p d) -> p b d", p=P, d=D))
+        nc.sync.dma_start(one_t[:], one[0, :].rearrange("(b p d) -> p b d", p=P, d=D))
+        with nc.allow_non_contiguous_dma(reason="one value a row"):
+            nc.sync.dma_start(scl_t[:], scl.rearrange("(b p) o -> p (b o)", p=P))
+
+        ident = keep.tile([P, P], F32, name="ident")
+        make_identity(nc, ident[:])
+
+        neg_lam = keep.tile([P, HALVES, D], F32, name="neg_lam")
+        cap = keep.tile([P, HALVES, D], F32, name="cap")
+        neg_cap = keep.tile([P, HALVES, D], F32, name="neg_cap")
+        cut_lam = keep.tile([P, HALVES, D], F32, name="cut_lam")
+        cut_pair = keep.tile([P, HALVES, 2], F32, name="cut_pair")
+        cut_sum = keep.tile([P, HALVES], F32, name="cut_sum")
+        half_scl = keep.tile([P, MB], F32, name="half_scl")
+        nc.gpsimd.tensor_scalar(neg_lam[:], lam_t[:], -1.0, 0.0, ALU.mult, ALU.add)
+        nc.gpsimd.tensor_scalar(cut_lam[:], lam_t[:], -CUT, 0.0, ALU.mult, ALU.add)
+        nc.gpsimd.tensor_tensor(cut_pair[:], cut_lam[:, :, 0:2], cut_lam[:, :, 2:4], ALU.add)
+        nc.gpsimd.tensor_tensor(cut_sum[:], cut_pair[:, :, 0], cut_pair[:, :, 1], ALU.add)
+        nc.gpsimd.tensor_scalar(cap[:], one_t[:], 1.0 / GAIN, CUT, ALU.mult, ALU.add)
+        nc.gpsimd.tensor_scalar(neg_cap[:], one_t[:], -1.0 / GAIN, -CUT, ALU.mult, ALU.add)
+        nc.gpsimd.tensor_scalar(half_scl[:], scl_t[:], 0.5, 0.0, ALU.mult, ALU.add)
+
+        w_codes = [keep.tile([P, N], U32, name="w_codes%d" % o, align_bytes=64) for o in range(PASSES)]
+        w_scales = [keep.tile([P, N], U8, name="w_scales%d" % o, align_bytes=64) for o in range(PASSES)]
+        w_bf = [keep.tile([P, N, PACK], BF16, name="w_bf%d" % o, align_bytes=64) for o in range(PASSES)]
+
+        picked_bytes = keep.tile([P, S], U8, name="picked_bytes", align_bytes=64)
+        x_sc = keep.tile([P, HALVES, D, P], U8, name="x_sc", align_bytes=64)
+        x_codes = [
+            [keep.tile([P, D, P], U32, name="x_codes%d_%d" % (o, b), align_bytes=64) for b in range(HALVES)]
+            for o in range(PASSES)
+        ]
+
+        def gather_words(o, b):
+            nc.vector.tensor_copy(
+                x_codes[o][b][:].rearrange("p d v -> p v d"),
+                word_win[o][:].indirect(offsets[:, b * HALF // 16 : (b + 1) * HALF // 16]),
+            )
+
+        def quantise_w(o):
+            nc.scalar.copy(w_bf[o][:], w_raw[o][:].rearrange("p j n -> p n j"))
+            nc.vector.quantize_mx(
+                out=w_codes[o][:].bitcast(FP8X4), scales=w_scales[o][:], in_=w_bf[o][:].rearrange("p n j -> p (n j)")
+            )
+
+        nc.vector.tensor_copy(picked_bytes[:, 0:HALF], scale_win[:].indirect(offsets[:, 0 : HALF // 16]))
+        nc.vector.tensor_copy(picked_bytes[:, HALF:S], scale_win[:].indirect(offsets[:, HALF // 16 : S // 16]))
+        nc.vector.tensor_copy(x_sc[:], picked_bytes[:].rearrange("p (b v d) -> p b d v", b=HALVES, d=D))
+        gather_words(0, 0)
+        gather_words(0, 1)
+        quantise_w(0)
+        quantise_w(1)
+
+        def bank_tile(slot):
+            return psum.tile([P, N], F32, name="bank%d" % slot, tag="bank%d" % slot)
+
+        y_bank = [[bank_tile(D * b + d) for d in range(D)] for b in range(HALVES)]
+        y_sb = [[keep.tile([P, N], F32, name="y_sb%d_%d" % (b, d)) for d in range(D)] for b in range(HALVES)]
+
+        def product(o, b):
+            for d in range(D):
+                nc.tensor.matmul_mx(
+                    out=y_bank[b][d][:],
+                    lhsT=x_codes[o][b][:, d, :].bitcast(FP8X4),
+                    lhsT_scale=x_sc[4 * o :, b, d, :],
+                    rhs=w_codes[o][:].bitcast(FP8X4),
+                    rhs_scale=w_scales[o][:],
+                    start=(o == 0),
+                    stop=(o == PASSES - 1),
+                )
+                if o == PASSES - 1:
+                    nc.scalar.copy(y_sb[b][d][:], y_bank[b][d][:])
+
+        def terms(b, kind):
+            made = []
+            for side in range(2):
+                made.append([keep.tile([P, N], F32, name="term%d_%d_%d_%d" % (b, kind, side, d)) for d in range(D)])
+            for d in range(D):
+                y = y_sb[b][d][:]
+                if kind == 0:
+                    nc.vector.tensor_scalar(made[0][d][:], y, CUT, cap[:, b, d : d + 1], ALU.max, ALU.min)
+                    nc.vector.tensor_scalar(made[1][d][:], y, -CUT, neg_cap[:, b, d : d + 1], ALU.min, ALU.max)
+                else:
+                    nc.vector.tensor_scalar(made[1][d][:], y, -CUT, neg_lam[:, b, d : d + 1], ALU.min, ALU.mult)
+                    nc.vector.tensor_scalar(made[0][d][:], y, CUT, lam_t[:, b, d : d + 1], ALU.max, ALU.mult)
+            return made
+
+        def sums(b, kind, made):
+            banks = [None, None]
+            for side in ((0, 1) if kind == 0 else (1, 0)):
+                bank = bank_tile(D * kind + 2 * b + side)
+                banks[side] = bank
+                for mb in range(MB):
+                    parts = [made[side][d][:, mb * P : (mb + 1) * P] for d in range(D)]
+                    if kind == 1:
+                        parts = [cut_sum[:, b : b + 1].to_broadcast([P, P])] + parts
+                    for i, part in enumerate(parts):
+                        nc.tensor.matmul(
+                            bank[:, mb * P : (mb + 1) * P], part, ident[:], start=(i == 0), stop=(i == len(parts) - 1), is_transpose=True
+                        )
+            return banks
+
+        root = [keep.tile([P, 2, N], F32, name="root%d" % b) for b in range(HALVES)]
+        recip = [keep.tile([P, 2, N], F32, name="recip%d" % b) for b in range(HALVES)]
+        warm2 = keep.tile([P, 1], F32, name="warm2")
+        shift = FLOOR - D * GAIN * CUT
+
+        def reciprocals(b, bank):
+            for side in range(2):
+                nc.scalar.activation(
+                    root[b][:, side, :],
+                    bank[side][:],
+                    ACT.Abs_reciprocal_sqrt,
+                    bias=shift,
+                    scale=GAIN if side == 0 else -GAIN,
+                )
+            if b == HALVES - 1:
+                nc.scalar.activation(warm2[:], root[b][:, 1, 0:1], ACT.Tanh)
+            nc.scalar.activation(recip[b][:], root[b][:], ACT.Square)
+
+        def finish(b, bank):
+            def tile(name):
+                return keep.tile([P, N], F32, name="%s%d" % (name, b))
+
+            pos = bank[0][:]
+            neg = tile("neg")
+            if b == 0:
+                nc.vector.tensor_copy(neg[:], bank[1][:])
+            else:
+                nc.scalar.copy(neg[:], bank[1][:])
+            diff, total, avg_p, avg_n, size = tile("diff"), tile("total"), tile("avg_p"), tile("avg_n"), tile("size")
+            nc.vector.tensor_tensor(diff[:], pos, neg[:], ALU.subtract)
+            nc.vector.tensor_tensor(total[:], pos, neg[:], ALU.add)
+            nc.vector.tensor_tensor(avg_p[:], pos, recip[b][:, 0, :], ALU.mult)
+            nc.vector.tensor_tensor(avg_n[:], neg[:], recip[b][:, 1, :], ALU.mult)
+            vote, damp = tile("vote")[:], tile("damp")[:]
+            nc.scalar.activation(vote, diff[:], ACT.Tanh, scale=3.0)
+            nc.scalar.activation(damp, total[:], ACT.Exp, scale=-1.0)
+            nc.scalar.activation(size[:], diff[:], ACT.Abs)
+            up, down, both, sided, res = tile("up"), tile("down"), tile("both"), tile("sided"), tile("res")
+            nc.vector.scalar_tensor_tensor(up[:], vote, 1.0, avg_p[:], ALU.add, ALU.mult)
+            nc.vector.scalar_tensor_tensor(down[:], vote, -1.0, avg_n[:], ALU.add, ALU.mult)
+            nc.vector.tensor_tensor(sided[:], size[:], damp, ALU.mult)
+            nc.vector.tensor_tensor(both[:], up[:], down[:], ALU.add)
+            for mb in range(MB):
+                cols = slice(mb * P, (mb + 1) * P)
+                nc.vector.scalar_tensor_tensor(
+                    res[:, cols], both[:, cols], half_scl[:, mb : mb + 1], sided[:, cols], ALU.mult, ALU.add
+                )
+            nc.sync.dma_start(
+                out[:, b * P : (b + 1) * P].rearrange("(a p) v -> p a v", p=P), res[:].rearrange("p (a v) -> p a v", a=MB)
+            )
+
+        product(0, 0)
+        product(0, 1)
+        gather_words(1, 0)
+        product(1, 0)
+        gather_words(1, 1)
+        product(1, 1)
+        counts0 = terms(0, 0)
+        count_bank0 = sums(0, 0, counts0)
+        reciprocals(0, count_bank0)
+        counts1 = terms(1, 0)
+        count_bank1 = sums(1, 0, counts1)
+        reciprocals(1, count_bank1)
+        loads0 = terms(0, 1)
+        load_bank0 = sums(0, 1, loads0)
+        loads1 = terms(1, 1)
+        load_bank1 = sums(1, 1, loads1)
+        finish(0, load_bank0)
+        finish(1, load_bank1)

@@ -8,12 +8,17 @@ FLOPS = 2 * K * S * N
 P = 128
 PACK = 4
 PASSES = K // (P * PACK)
-HALVES = S // (P * D)
+QUADRANTS = 4
+SCALE_ROWS = 4
+PER_COLUMN = 16
 HALF = P * D
-MB = N // P
+HALVES = S // HALF
+ROW_BLOCKS = N // P
 CUT = 0.3
 GAIN = 4.0
 FLOOR = 0.3
+SHARPNESS = 6.0
+POS, NEG = 0, 1
 
 F32 = mybir.dt.float32
 BF16 = mybir.dt.bfloat16
@@ -24,7 +29,6 @@ U8 = mybir.dt.uint8
 FP8X4 = mybir.dt.float8_e4m3fn_x4
 ALU = mybir.AluOpType
 ACT = mybir.ActivationFunctionType
-AX = mybir.AxisListType
 
 
 def tile_picked_ytiesm_dis_p_kernel(tc, x_words, x_scales, w1, lam, one, scl, offs, out):
@@ -33,204 +37,222 @@ def tile_picked_ytiesm_dis_p_kernel(tc, x_words, x_scales, w1, lam, one, scl, of
         keep = ctx.enter_context(tc.tile_pool(name="keep", bufs=1))
         psum = ctx.enter_context(tc.psum_pool(name="psum", bufs=1))
 
-        offsets = keep.tile([P, S // 16], U16, name="offsets")
+        offsets = keep.tile([P, S // PER_COLUMN], U16, name="offsets")
         nc.sync.dma_start(offsets[:], offs)
+        lam_t = keep.tile([P, HALVES, D], F32, name="lam_t")
+        one_t = keep.tile([P, HALVES, D], F32, name="one_t")
+        scl_t = keep.tile([P, ROW_BLOCKS], F32, name="scl_t")
+        nc.sync.dma_start(lam_t[:], lam[0, :].rearrange("(h v d) -> v h d", v=P, d=D))
+        nc.sync.dma_start(one_t[:], one[0, :].rearrange("(h v d) -> v h d", v=P, d=D))
 
-        scale_win = keep.tile([P, T], U8, name="scale_win", align_bytes=64)
-        nc.vector.memset(scale_win[:].bitcast(I32), 0)
-        for q in range(4):
-            nc.scalar.dma_start(
-                scale_win[32 * q : 32 * q + 4 * PASSES, :].bitcast(I32),
-                x_scales[:, 4 * q : 4 * q + 4, :].bitcast(I32),
+        scale_table = keep.tile([P, T], U8, name="scale_table", align_bytes=64)
+        nc.vector.memset(scale_table[:, : T // 2].bitcast(I32), 0)
+        nc.gpsimd.memset(scale_table[:, T // 2 :].bitcast(I32), 0)
+        for q in range(QUADRANTS):
+            nc.sync.dma_start(
+                scale_table[32 * q : 32 * q + SCALE_ROWS * PASSES, :].bitcast(I32),
+                x_scales[:, SCALE_ROWS * q : SCALE_ROWS * (q + 1), :].bitcast(I32),
             )
 
-        warm = keep.tile([P, 2], F32, name="warm")
-        nc.vector.memset(warm[:, 0:1], 1.0)
-        nc.scalar.activation(warm[:, 1:2], warm[:, 0:1], ACT.Abs_reciprocal_sqrt)
-
-        word_win = [keep.tile([P, T], U32, name="word_win%d" % o, align_bytes=64) for o in range(PASSES)]
+        word_table = [keep.tile([P, T], U32, name="word_table%d" % o, align_bytes=64) for o in range(PASSES)]
         w_raw = [keep.tile([P, PACK, N], F32, name="w_raw%d" % o) for o in range(PASSES)]
 
         def load_words(o):
-            nc.sync.dma_start(word_win[o][:].bitcast(I32), x_words[o].rearrange("p n t -> p (n t)").bitcast(I32))
+            nc.sync.dma_start(word_table[o][:].bitcast(I32), x_words[o].rearrange("p n t -> p (n t)").bitcast(I32))
 
         load_words(0)
         for o in range(PASSES):
-            nc.sync.dma_start(w_raw[o][:], w1[o * P * PACK : (o + 1) * P * PACK, :].rearrange("(p j) n -> p j n", j=PACK))
+            nc.sync.dma_start(w_raw[o][:], w1[o * P * PACK : (o + 1) * P * PACK, :].rearrange("(p t) n -> p t n", t=PACK))
         load_words(1)
 
-        lam_t = keep.tile([P, HALVES, D], F32, name="lam_t")
-        one_t = keep.tile([P, HALVES, D], F32, name="one_t")
-        scl_t = keep.tile([P, MB], F32, name="scl_t")
-        nc.sync.dma_start(lam_t[:], lam[0, :].rearrange("(b p d) -> p b d", p=P, d=D))
-        nc.sync.dma_start(one_t[:], one[0, :].rearrange("(b p d) -> p b d", p=P, d=D))
-        with nc.allow_non_contiguous_dma(reason="one value a row"):
-            nc.sync.dma_start(scl_t[:], scl.rearrange("(b p) o -> p (b o)", p=P))
+        with nc.allow_non_contiguous_dma(reason="one value for each output row"):
+            nc.sync.dma_start(scl_t[:], scl.rearrange("(r p) o -> p (r o)", p=P))
 
         ident = keep.tile([P, P], F32, name="ident")
         make_identity(nc, ident[:])
 
         neg_lam = keep.tile([P, HALVES, D], F32, name="neg_lam")
-        cap = keep.tile([P, HALVES, D], F32, name="cap")
+        pos_cap = keep.tile([P, HALVES, D], F32, name="pos_cap")
         neg_cap = keep.tile([P, HALVES, D], F32, name="neg_cap")
         cut_lam = keep.tile([P, HALVES, D], F32, name="cut_lam")
-        cut_pair = keep.tile([P, HALVES, 2], F32, name="cut_pair")
         cut_sum = keep.tile([P, HALVES], F32, name="cut_sum")
-        half_scl = keep.tile([P, MB], F32, name="half_scl")
-        nc.gpsimd.tensor_scalar(neg_lam[:], lam_t[:], -1.0, 0.0, ALU.mult, ALU.add)
-        nc.gpsimd.tensor_scalar(cut_lam[:], lam_t[:], -CUT, 0.0, ALU.mult, ALU.add)
-        nc.gpsimd.tensor_tensor(cut_pair[:], cut_lam[:, :, 0:2], cut_lam[:, :, 2:4], ALU.add)
-        nc.gpsimd.tensor_tensor(cut_sum[:], cut_pair[:, :, 0], cut_pair[:, :, 1], ALU.add)
-        nc.gpsimd.tensor_scalar(cap[:], one_t[:], 1.0 / GAIN, CUT, ALU.mult, ALU.add)
-        nc.gpsimd.tensor_scalar(neg_cap[:], one_t[:], -1.0 / GAIN, -CUT, ALU.mult, ALU.add)
-        nc.gpsimd.tensor_scalar(half_scl[:], scl_t[:], 0.5, 0.0, ALU.mult, ALU.add)
+        half_scl = keep.tile([P, ROW_BLOCKS], F32, name="half_scl")
 
         w_codes = [keep.tile([P, N], U32, name="w_codes%d" % o, align_bytes=64) for o in range(PASSES)]
         w_scales = [keep.tile([P, N], U8, name="w_scales%d" % o, align_bytes=64) for o in range(PASSES)]
-        w_bf = [keep.tile([P, N, PACK], BF16, name="w_bf%d" % o, align_bytes=64) for o in range(PASSES)]
+        w_bf = [keep.tile([P, N, PACK], BF16, name="w_bf%d" % o, tag="w_bf%d" % o, align_bytes=64) for o in range(PASSES)]
 
         picked_bytes = keep.tile([P, S], U8, name="picked_bytes", align_bytes=64)
         x_sc = keep.tile([P, HALVES, D, P], U8, name="x_sc", align_bytes=64)
-        x_codes = [
-            [keep.tile([P, D, P], U32, name="x_codes%d_%d" % (o, b), align_bytes=64) for b in range(HALVES)]
-            for o in range(PASSES)
-        ]
+        x_codes = [[None] * HALVES for o in range(PASSES)]
 
-        def gather_words(o, b):
+        def gather_words(o, h, tag):
+            x_codes[o][h] = keep.tile([P, D, P], U32, name="x_codes%d_%d" % (o, h), tag=tag, align_bytes=64)
             nc.vector.tensor_copy(
-                x_codes[o][b][:].rearrange("p d v -> p v d"),
-                word_win[o][:].indirect(offsets[:, b * HALF // 16 : (b + 1) * HALF // 16]),
+                x_codes[o][h][:].rearrange("p d v -> p v d"),
+                word_table[o][:].indirect(offsets[:, h * HALF // PER_COLUMN : (h + 1) * HALF // PER_COLUMN]),
             )
 
         def quantise_w(o):
-            nc.scalar.copy(w_bf[o][:], w_raw[o][:].rearrange("p j n -> p n j"))
+            nc.scalar.copy(
+                w_bf[o][:].rearrange("p (c i) t -> p c t i", i=PACK), w_raw[o][:].rearrange("p t (c i) -> p c t i", i=PACK)
+            )
             nc.vector.quantize_mx(
-                out=w_codes[o][:].bitcast(FP8X4), scales=w_scales[o][:], in_=w_bf[o][:].rearrange("p n j -> p (n j)")
+                out=w_codes[o][:].bitcast(FP8X4), scales=w_scales[o][:], in_=w_bf[o][:].rearrange("p n t -> p (n t)")
             )
 
-        nc.vector.tensor_copy(picked_bytes[:, 0:HALF], scale_win[:].indirect(offsets[:, 0 : HALF // 16]))
-        nc.vector.tensor_copy(picked_bytes[:, HALF:S], scale_win[:].indirect(offsets[:, HALF // 16 : S // 16]))
-        nc.vector.tensor_copy(x_sc[:], picked_bytes[:].rearrange("p (b v d) -> p b d v", b=HALVES, d=D))
-        gather_words(0, 0)
-        gather_words(0, 1)
+        nc.vector.tensor_copy(picked_bytes[:], scale_table[:].indirect(offsets[:]))
+        nc.vector.tensor_copy(x_sc[:], picked_bytes[:].rearrange("p (h v d) -> p h d v", h=HALVES, d=D))
+        gather_words(0, 0, "x_codes0_0")
         quantise_w(0)
         quantise_w(1)
+
+        nc.scalar.activation(pos_cap[:], one_t[:], ACT.Copy, scale=1.0 / GAIN)
+        nc.scalar.activation(neg_cap[:], one_t[:], ACT.Copy, bias=-2 * CUT, scale=-1.0 / GAIN)
+        nc.scalar.activation(neg_lam[:], lam_t[:], ACT.Copy, scale=-1.0)
+        for h in range(HALVES):
+            nc.scalar.activation(cut_lam[:, h, :], lam_t[:, h, :], ACT.Copy, scale=-2 * CUT, accum_out=cut_sum[:, h : h + 1])
+        nc.scalar.activation(half_scl[:], scl_t[:], ACT.Copy, scale=0.5)
 
         def bank_tile(slot):
             return psum.tile([P, N], F32, name="bank%d" % slot, tag="bank%d" % slot)
 
-        y_bank = [[bank_tile(D * b + d) for d in range(D)] for b in range(HALVES)]
-        y_sb = [[keep.tile([P, N], F32, name="y_sb%d_%d" % (b, d)) for d in range(D)] for b in range(HALVES)]
+        def row_tile(name, h):
+            return keep.tile([P, N], F32, name="%s%d" % (name, h))
 
-        def product(o, b):
+        y_bank = [[bank_tile(D * h + d) for d in range(D)] for h in range(HALVES)]
+        z = [[keep.tile([P, N], F32, name="z%d_%d" % (h, d)) for d in range(D)] for h in range(HALVES)]
+
+        def product(o, h):
             for d in range(D):
                 nc.tensor.matmul_mx(
-                    out=y_bank[b][d][:],
-                    lhsT=x_codes[o][b][:, d, :].bitcast(FP8X4),
-                    lhsT_scale=x_sc[4 * o :, b, d, :],
+                    out=y_bank[h][d][:],
+                    lhsT=x_codes[o][h][:, d, :].bitcast(FP8X4),
+                    lhsT_scale=x_sc[SCALE_ROWS * o :, h, d, :],
                     rhs=w_codes[o][:].bitcast(FP8X4),
                     rhs_scale=w_scales[o][:],
                     start=(o == 0),
                     stop=(o == PASSES - 1),
                 )
                 if o == PASSES - 1:
-                    nc.scalar.copy(y_sb[b][d][:], y_bank[b][d][:])
+                    nc.scalar.activation(z[h][d][:], y_bank[h][d][:], ACT.Copy, bias=-CUT)
 
-        def terms(b, kind):
-            made = []
-            for side in range(2):
-                made.append([keep.tile([P, N], F32, name="term%d_%d_%d_%d" % (b, kind, side, d)) for d in range(D)])
+        weighted = [
+            [[keep.tile([P, N], F32, name="term%d_%d_%d" % (h, side, d)) for d in range(D)] for side in (POS, NEG)]
+            for h in range(HALVES)
+        ]
+        counted = [[weighted[0][NEG], weighted[1][POS]], [z[0], weighted[1][POS]]]
+
+        def weigh_terms(h):
             for d in range(D):
-                y = y_sb[b][d][:]
-                if kind == 0:
-                    nc.vector.tensor_scalar(made[0][d][:], y, CUT, cap[:, b, d : d + 1], ALU.max, ALU.min)
-                    nc.vector.tensor_scalar(made[1][d][:], y, -CUT, neg_cap[:, b, d : d + 1], ALU.min, ALU.max)
-                else:
-                    nc.vector.tensor_scalar(made[1][d][:], y, -CUT, neg_lam[:, b, d : d + 1], ALU.min, ALU.mult)
-                    nc.vector.tensor_scalar(made[0][d][:], y, CUT, lam_t[:, b, d : d + 1], ALU.max, ALU.mult)
-            return made
-
-        def sums(b, kind, made):
-            banks = [None, None]
-            for side in ((0, 1) if kind == 0 else (1, 0)):
-                bank = bank_tile(D * kind + 2 * b + side)
-                banks[side] = bank
-                for mb in range(MB):
-                    parts = [made[side][d][:, mb * P : (mb + 1) * P] for d in range(D)]
-                    if kind == 1:
-                        parts = [cut_sum[:, b : b + 1].to_broadcast([P, P])] + parts
-                    for i, part in enumerate(parts):
-                        nc.tensor.matmul(
-                            bank[:, mb * P : (mb + 1) * P], part, ident[:], start=(i == 0), stop=(i == len(parts) - 1), is_transpose=True
-                        )
-            return banks
-
-        root = [keep.tile([P, 2, N], F32, name="root%d" % b) for b in range(HALVES)]
-        recip = [keep.tile([P, 2, N], F32, name="recip%d" % b) for b in range(HALVES)]
-        warm2 = keep.tile([P, 1], F32, name="warm2")
-        shift = FLOOR - D * GAIN * CUT
-
-        def reciprocals(b, bank):
-            for side in range(2):
-                nc.scalar.activation(
-                    root[b][:, side, :],
-                    bank[side][:],
-                    ACT.Abs_reciprocal_sqrt,
-                    bias=shift,
-                    scale=GAIN if side == 0 else -GAIN,
+                nc.vector.tensor_scalar(
+                    weighted[h][NEG][d][:], z[h][d][:], -2 * CUT, neg_lam[:, h, d : d + 1], ALU.min, ALU.mult
                 )
-            if b == HALVES - 1:
-                nc.scalar.activation(warm2[:], root[b][:, 1, 0:1], ACT.Tanh)
-            nc.scalar.activation(recip[b][:], root[b][:], ACT.Square)
+                nc.vector.tensor_scalar(weighted[h][POS][d][:], z[h][d][:], 0.0, lam_t[:, h, d : d + 1], ALU.max, ALU.mult)
 
-        def finish(b, bank):
-            def tile(name):
-                return keep.tile([P, N], F32, name="%s%d" % (name, b))
-
-            pos = bank[0][:]
-            neg = tile("neg")
-            if b == 0:
-                nc.vector.tensor_copy(neg[:], bank[1][:])
-            else:
-                nc.scalar.copy(neg[:], bank[1][:])
-            diff, total, avg_p, avg_n, size = tile("diff"), tile("total"), tile("avg_p"), tile("avg_n"), tile("size")
-            nc.vector.tensor_tensor(diff[:], pos, neg[:], ALU.subtract)
-            nc.vector.tensor_tensor(total[:], pos, neg[:], ALU.add)
-            nc.vector.tensor_tensor(avg_p[:], pos, recip[b][:, 0, :], ALU.mult)
-            nc.vector.tensor_tensor(avg_n[:], neg[:], recip[b][:, 1, :], ALU.mult)
-            vote, damp = tile("vote")[:], tile("damp")[:]
-            nc.scalar.activation(vote, diff[:], ACT.Tanh, scale=3.0)
-            nc.scalar.activation(damp, total[:], ACT.Exp, scale=-1.0)
-            nc.scalar.activation(size[:], diff[:], ACT.Abs)
-            up, down, both, sided, res = tile("up"), tile("down"), tile("both"), tile("sided"), tile("res")
-            nc.vector.scalar_tensor_tensor(up[:], vote, 1.0, avg_p[:], ALU.add, ALU.mult)
-            nc.vector.scalar_tensor_tensor(down[:], vote, -1.0, avg_n[:], ALU.add, ALU.mult)
-            nc.vector.tensor_tensor(sided[:], size[:], damp, ALU.mult)
-            nc.vector.tensor_tensor(both[:], up[:], down[:], ALU.add)
-            for mb in range(MB):
-                cols = slice(mb * P, (mb + 1) * P)
-                nc.vector.scalar_tensor_tensor(
-                    res[:, cols], both[:, cols], half_scl[:, mb : mb + 1], sided[:, cols], ALU.mult, ALU.add
+        def count_terms(h):
+            for d in range(D):
+                nc.vector.tensor_scalar(counted[h][POS][d][:], z[h][d][:], 0.0, pos_cap[:, h, d : d + 1], ALU.max, ALU.min)
+            for d in range(D):
+                nc.vector.tensor_scalar(
+                    counted[h][NEG][d][:], z[h][d][:], -2 * CUT, neg_cap[:, h, d : d + 1], ALU.min, ALU.max
                 )
+
+        def member_sum(slot, members, column=None):
+            bank = bank_tile(slot)
+            for r in range(ROW_BLOCKS):
+                rows = slice(r * P, (r + 1) * P)
+                parts = [member[:, rows] for member in members]
+                if column is not None:
+                    parts = [column.to_broadcast([P, P])] + parts
+                for i, part in enumerate(parts):
+                    nc.tensor.matmul(
+                        bank[:, rows], part, ident[:], start=(i == 0), stop=(i == len(parts) - 1), is_transpose=True
+                    )
+            return bank
+
+        def per_half(name):
+            return [row_tile(name, h) for h in range(HALVES)]
+
+        def both_halves(name):
+            return keep.tile([P, HALVES, N], F32, name=name)
+
+        diff, total = per_half("diff"), per_half("total")
+        nsum, vote, damp, size, down = [both_halves(name) for name in ("nsum", "vote", "damp", "size", "down")]
+        sided = [counted[0][POS][1], row_tile("sided", 1)]
+        up = [counted[0][POS][0], row_tile("up", 1)]
+        partial, result = per_half("partial"), per_half("result")
+        root = [[total[1], total[1]], [row_tile("root_p", 1), row_tile("root_n", 1)]]
+        recip = [[row_tile("recip_p", h), row_tile("recip_n", h)] for h in range(HALVES)]
+        count_scale = [GAIN, -GAIN]
+        count_bias = [FLOOR, FLOOR - D * GAIN * 2 * CUT]
+
+        def elect(h, banks):
+            nc.scalar.copy(nsum[:, h, :], banks[NEG][:])
+            nc.vector.tensor_tensor(diff[h][:], banks[POS][:], nsum[:, h, :], ALU.subtract)
+            nc.vector.tensor_tensor(total[h][:], banks[POS][:], nsum[:, h, :], ALU.add)
+            nc.scalar.activation(vote[:, h, :], diff[h][:], ACT.Tanh, scale=SHARPNESS / 2)
+            nc.scalar.activation(damp[:, h, :], total[h][:], ACT.Exp, scale=-1.0)
+
+        def absolute(h):
+            nc.scalar.activation(size[:, h, :], diff[h][:], ACT.Abs)
+
+        def one_sidedness(h):
+            nc.vector.tensor_tensor(sided[h][:], size[:, h, :], damp[:, h, :], ALU.mult)
+
+        def reciprocal(h, side, bank):
+            nc.scalar.activation(
+                root[h][side][:], bank[:], ACT.Abs_reciprocal_sqrt, bias=count_bias[side], scale=count_scale[side]
+            )
+            nc.scalar.activation(recip[h][side][:], root[h][side][:], ACT.Square)
+
+        def finish(h):
+            steps = ((POS, up[h][:], sided[h][:], partial[h][:]), (NEG, down[:, h, :], partial[h][:], result[h][:]))
+            for side, elected, before, after in steps:
+                scaled = row_tile("scaled%d_" % side, h)
+                for r in range(ROW_BLOCKS):
+                    rows = slice(r * P, (r + 1) * P)
+                    nc.vector.scalar_tensor_tensor(
+                        scaled[:, rows], elected[:, rows], half_scl[:, r : r + 1], recip[h][side][:, rows], ALU.mult, ALU.mult
+                    )
+                nc.vector.tensor_tensor(after, before, scaled[:], ALU.add)
             nc.sync.dma_start(
-                out[:, b * P : (b + 1) * P].rearrange("(a p) v -> p a v", p=P), res[:].rearrange("p (a v) -> p a v", a=MB)
+                out[:, h * P : (h + 1) * P].rearrange("(r p) v -> p r v", p=P),
+                result[h][:].rearrange("p (r v) -> p r v", r=ROW_BLOCKS),
             )
 
         product(0, 0)
-        product(0, 1)
-        gather_words(1, 0)
+        gather_words(1, 0, "x_codes1_0")
         product(1, 0)
-        gather_words(1, 1)
+        gather_words(0, 1, "w_bf0")
+        product(0, 1)
+        gather_words(1, 1, "x_codes1_1")
         product(1, 1)
-        counts0 = terms(0, 0)
-        count_bank0 = sums(0, 0, counts0)
-        reciprocals(0, count_bank0)
-        counts1 = terms(1, 0)
-        count_bank1 = sums(1, 0, counts1)
-        reciprocals(1, count_bank1)
-        loads0 = terms(0, 1)
-        load_bank0 = sums(0, 1, loads0)
-        loads1 = terms(1, 1)
-        load_bank1 = sums(1, 1, loads1)
-        finish(0, load_bank0)
-        finish(1, load_bank1)
+
+        sum_banks = []
+        for h in range(HALVES):
+            weigh_terms(h)
+            neg_bank = member_sum(2 * h + NEG, weighted[h][NEG], cut_sum[:, h : h + 1])
+            pos_bank = member_sum(2 * h + POS, weighted[h][POS])
+            sum_banks.append([pos_bank, neg_bank])
+        elect(0, sum_banks[0])
+        absolute(0)
+        elect(1, sum_banks[1])
+        count_banks = []
+        for h in range(HALVES):
+            count_terms(h)
+            count_banks.append([member_sum(D + 2 * h + side, counted[h][side]) for side in (POS, NEG)])
+
+        for h in range(HALVES):
+            nc.vector.scalar_tensor_tensor(up[h][:], vote[:, h, :], 1.0, sum_banks[h][POS][:], ALU.add, ALU.mult)
+        one_sidedness(0)
+        nc.vector.scalar_tensor_tensor(down[:], vote[:], -1.0, nsum[:], ALU.add, ALU.mult)
+
+        reciprocal(0, POS, count_banks[0][POS])
+        absolute(1)
+        reciprocal(0, NEG, count_banks[0][NEG])
+        finish(0)
+        for side in (POS, NEG):
+            reciprocal(1, side, count_banks[1][side])
+        one_sidedness(1)
+        finish(1)

from contextlib import ExitStack

import concourse.mybir as mybir
from concourse.masks import make_identity

K, T, S, D, N = 1024, 2048, 1024, 4, 256
FLOPS = 2 * K * S * N
P = 128
PACK = 4
PASSES = K // (P * PACK)
QUADRANTS = 4
SCALE_ROWS = 4
PER_COLUMN = 16
HALF = P * D
HALVES = S // HALF
ROW_BLOCKS = N // P
CUT = 0.3
GAIN = 4.0
FLOOR = 0.3
SHARPNESS = 6.0
POS, NEG = 0, 1

F32 = mybir.dt.float32
BF16 = mybir.dt.bfloat16
I32 = mybir.dt.int32
U32 = mybir.dt.uint32
U16 = mybir.dt.uint16
U8 = mybir.dt.uint8
FP8X4 = mybir.dt.float8_e4m3fn_x4
ALU = mybir.AluOpType
ACT = mybir.ActivationFunctionType


def tile_picked_ytiesm_dis_p_kernel(tc, x_words, x_scales, w1, lam, one, scl, offs, out):
    nc = tc.nc
    with ExitStack() as ctx:
        keep = ctx.enter_context(tc.tile_pool(name="keep", bufs=1))
        psum = ctx.enter_context(tc.psum_pool(name="psum", bufs=1))

        offsets = keep.tile([P, S // PER_COLUMN], U16, name="offsets")
        nc.sync.dma_start(offsets[:], offs)
        lam_t = keep.tile([P, HALVES, D], F32, name="lam_t")
        one_t = keep.tile([P, HALVES, D], F32, name="one_t")
        scl_t = keep.tile([P, ROW_BLOCKS], F32, name="scl_t")
        nc.sync.dma_start(lam_t[:], lam[0, :].rearrange("(h v d) -> v h d", v=P, d=D))
        nc.sync.dma_start(one_t[:], one[0, :].rearrange("(h v d) -> v h d", v=P, d=D))

        scale_table = keep.tile([P, T], U8, name="scale_table", align_bytes=64)
        nc.vector.memset(scale_table[:, : T // 2].bitcast(I32), 0)
        nc.gpsimd.memset(scale_table[:, T // 2 :].bitcast(I32), 0)
        for q in range(QUADRANTS):
            nc.sync.dma_start(
                scale_table[32 * q : 32 * q + SCALE_ROWS * PASSES, :].bitcast(I32),
                x_scales[:, SCALE_ROWS * q : SCALE_ROWS * (q + 1), :].bitcast(I32),
            )

        word_table = [keep.tile([P, T], U32, name="word_table%d" % o, align_bytes=64) for o in range(PASSES)]
        w_raw = [keep.tile([P, PACK, N], F32, name="w_raw%d" % o) for o in range(PASSES)]

        def load_words(o):
            nc.sync.dma_start(word_table[o][:].bitcast(I32), x_words[o].rearrange("p n t -> p (n t)").bitcast(I32))

        load_words(0)
        for o in range(PASSES):
            nc.sync.dma_start(w_raw[o][:], w1[o * P * PACK : (o + 1) * P * PACK, :].rearrange("(p t) n -> p t n", t=PACK))
        load_words(1)

        with nc.allow_non_contiguous_dma(reason="one value for each output row"):
            nc.sync.dma_start(scl_t[:], scl.rearrange("(r p) o -> p (r o)", p=P))

        ident = keep.tile([P, P], F32, name="ident")
        make_identity(nc, ident[:])

        neg_lam = keep.tile([P, HALVES, D], F32, name="neg_lam")
        pos_cap = keep.tile([P, HALVES, D], F32, name="pos_cap")
        neg_cap = keep.tile([P, HALVES, D], F32, name="neg_cap")
        cut_lam = keep.tile([P, HALVES, D], F32, name="cut_lam")
        cut_sum = keep.tile([P, HALVES], F32, name="cut_sum")
        half_scl = keep.tile([P, ROW_BLOCKS], F32, name="half_scl")

        w_codes = [keep.tile([P, N], U32, name="w_codes%d" % o, align_bytes=64) for o in range(PASSES)]
        w_scales = [keep.tile([P, N], U8, name="w_scales%d" % o, align_bytes=64) for o in range(PASSES)]
        w_bf = [keep.tile([P, N, PACK], BF16, name="w_bf%d" % o, tag="w_bf%d" % o, align_bytes=64) for o in range(PASSES)]

        picked_bytes = keep.tile([P, S], U8, name="picked_bytes", align_bytes=64)
        x_sc = keep.tile([P, HALVES, D, P], U8, name="x_sc", align_bytes=64)
        x_codes = [[None] * HALVES for o in range(PASSES)]

        def gather_words(o, h, tag):
            x_codes[o][h] = keep.tile([P, D, P], U32, name="x_codes%d_%d" % (o, h), tag=tag, align_bytes=64)
            nc.vector.tensor_copy(
                x_codes[o][h][:].rearrange("p d v -> p v d"),
                word_table[o][:].indirect(offsets[:, h * HALF // PER_COLUMN : (h + 1) * HALF // PER_COLUMN]),
            )

        def quantise_w(o):
            nc.scalar.copy(
                w_bf[o][:].rearrange("p (c i) t -> p c t i", i=PACK), w_raw[o][:].rearrange("p t (c i) -> p c t i", i=PACK)
            )
            nc.vector.quantize_mx(
                out=w_codes[o][:].bitcast(FP8X4), scales=w_scales[o][:], in_=w_bf[o][:].rearrange("p n t -> p (n t)")
            )

        nc.vector.tensor_copy(picked_bytes[:], scale_table[:].indirect(offsets[:]))
        nc.vector.tensor_copy(x_sc[:], picked_bytes[:].rearrange("p (h v d) -> p h d v", h=HALVES, d=D))
        gather_words(0, 0, "x_codes0_0")
        quantise_w(0)
        quantise_w(1)

        nc.scalar.activation(pos_cap[:], one_t[:], ACT.Copy, scale=1.0 / GAIN)
        nc.scalar.activation(neg_cap[:], one_t[:], ACT.Copy, bias=-2 * CUT, scale=-1.0 / GAIN)
        nc.scalar.activation(neg_lam[:], lam_t[:], ACT.Copy, scale=-1.0)
        for h in range(HALVES):
            nc.scalar.activation(cut_lam[:, h, :], lam_t[:, h, :], ACT.Copy, scale=-2 * CUT, accum_out=cut_sum[:, h : h + 1])
        nc.scalar.activation(half_scl[:], scl_t[:], ACT.Copy, scale=0.5)

        def bank_tile(slot):
            return psum.tile([P, N], F32, name="bank%d" % slot, tag="bank%d" % slot)

        def row_tile(name, h):
            return keep.tile([P, N], F32, name="%s%d" % (name, h))

        y_bank = [[bank_tile(D * h + d) for d in range(D)] for h in range(HALVES)]
        z = [[keep.tile([P, N], F32, name="z%d_%d" % (h, d)) for d in range(D)] for h in range(HALVES)]

        def product(o, h):
            for d in range(D):
                nc.tensor.matmul_mx(
                    out=y_bank[h][d][:],
                    lhsT=x_codes[o][h][:, d, :].bitcast(FP8X4),
                    lhsT_scale=x_sc[SCALE_ROWS * o :, h, d, :],
                    rhs=w_codes[o][:].bitcast(FP8X4),
                    rhs_scale=w_scales[o][:],
                    start=(o == 0),
                    stop=(o == PASSES - 1),
                )
                if o == PASSES - 1:
                    nc.scalar.activation(z[h][d][:], y_bank[h][d][:], ACT.Copy, bias=-CUT)

        weighted = [
            [[keep.tile([P, N], F32, name="term%d_%d_%d" % (h, side, d)) for d in range(D)] for side in (POS, NEG)]
            for h in range(HALVES)
        ]
        counted = [[weighted[0][NEG], weighted[1][POS]], [z[0], weighted[1][POS]]]

        def weigh_terms(h):
            for d in range(D):
                nc.vector.tensor_scalar(
                    weighted[h][NEG][d][:], z[h][d][:], -2 * CUT, neg_lam[:, h, d : d + 1], ALU.min, ALU.mult
                )
                nc.vector.tensor_scalar(weighted[h][POS][d][:], z[h][d][:], 0.0, lam_t[:, h, d : d + 1], ALU.max, ALU.mult)

        def count_terms(h):
            for d in range(D):
                nc.vector.tensor_scalar(counted[h][POS][d][:], z[h][d][:], 0.0, pos_cap[:, h, d : d + 1], ALU.max, ALU.min)
            for d in range(D):
                nc.vector.tensor_scalar(
                    counted[h][NEG][d][:], z[h][d][:], -2 * CUT, neg_cap[:, h, d : d + 1], ALU.min, ALU.max
                )

        def member_sum(slot, members, column=None):
            bank = bank_tile(slot)
            for r in range(ROW_BLOCKS):
                rows = slice(r * P, (r + 1) * P)
                parts = [member[:, rows] for member in members]
                if column is not None:
                    parts = [column.to_broadcast([P, P])] + parts
                for i, part in enumerate(parts):
                    nc.tensor.matmul(
                        bank[:, rows], part, ident[:], start=(i == 0), stop=(i == len(parts) - 1), is_transpose=True
                    )
            return bank

        def per_half(name):
            return [row_tile(name, h) for h in range(HALVES)]

        def both_halves(name):
            return keep.tile([P, HALVES, N], F32, name=name)

        diff, total = per_half("diff"), per_half("total")
        nsum, vote, damp, size, down = [both_halves(name) for name in ("nsum", "vote", "damp", "size", "down")]
        sided = [counted[0][POS][1], row_tile("sided", 1)]
        up = [counted[0][POS][0], row_tile("up", 1)]
        partial, result = per_half("partial"), per_half("result")
        root = [[total[1], total[1]], [row_tile("root_p", 1), row_tile("root_n", 1)]]
        recip = [[row_tile("recip_p", h), row_tile("recip_n", h)] for h in range(HALVES)]
        count_scale = [GAIN, -GAIN]
        count_bias = [FLOOR, FLOOR - D * GAIN * 2 * CUT]

        def elect(h, banks):
            nc.scalar.copy(nsum[:, h, :], banks[NEG][:])
            nc.vector.tensor_tensor(diff[h][:], banks[POS][:], nsum[:, h, :], ALU.subtract)
            nc.vector.tensor_tensor(total[h][:], banks[POS][:], nsum[:, h, :], ALU.add)
            nc.scalar.activation(vote[:, h, :], diff[h][:], ACT.Tanh, scale=SHARPNESS / 2)
            nc.scalar.activation(damp[:, h, :], total[h][:], ACT.Exp, scale=-1.0)

        def absolute(h):
            nc.scalar.activation(size[:, h, :], diff[h][:], ACT.Abs)

        def one_sidedness(h):
            nc.vector.tensor_tensor(sided[h][:], size[:, h, :], damp[:, h, :], ALU.mult)

        def reciprocal(h, side, bank):
            nc.scalar.activation(
                root[h][side][:], bank[:], ACT.Abs_reciprocal_sqrt, bias=count_bias[side], scale=count_scale[side]
            )
            nc.scalar.activation(recip[h][side][:], root[h][side][:], ACT.Square)

        def finish(h):
            steps = ((POS, up[h][:], sided[h][:], partial[h][:]), (NEG, down[:, h, :], partial[h][:], result[h][:]))
            for side, elected, before, after in steps:
                scaled = row_tile("scaled%d_" % side, h)
                for r in range(ROW_BLOCKS):
                    rows = slice(r * P, (r + 1) * P)
                    nc.vector.scalar_tensor_tensor(
                        scaled[:, rows], elected[:, rows], half_scl[:, r : r + 1], recip[h][side][:, rows], ALU.mult, ALU.mult
                    )
                nc.vector.tensor_tensor(after, before, scaled[:], ALU.add)
            nc.sync.dma_start(
                out[:, h * P : (h + 1) * P].rearrange("(r p) v -> p r v", p=P),
                result[h][:].rearrange("p (r v) -> p r v", r=ROW_BLOCKS),
            )

        product(0, 0)
        gather_words(1, 0, "x_codes1_0")
        product(1, 0)
        gather_words(0, 1, "w_bf0")
        product(0, 1)
        gather_words(1, 1, "x_codes1_1")
        product(1, 1)

        sum_banks = []
        for h in range(HALVES):
            weigh_terms(h)
            neg_bank = member_sum(2 * h + NEG, weighted[h][NEG], cut_sum[:, h : h + 1])
            pos_bank = member_sum(2 * h + POS, weighted[h][POS])
            sum_banks.append([pos_bank, neg_bank])
        elect(0, sum_banks[0])
        absolute(0)
        elect(1, sum_banks[1])
        count_banks = []
        for h in range(HALVES):
            count_terms(h)
            count_banks.append([member_sum(D + 2 * h + side, counted[h][side]) for side in (POS, NEG)])

        for h in range(HALVES):
            nc.vector.scalar_tensor_tensor(up[h][:], vote[:, h, :], 1.0, sum_banks[h][POS][:], ALU.add, ALU.mult)
        one_sidedness(0)
        nc.vector.scalar_tensor_tensor(down[:], vote[:], -1.0, nsum[:], ALU.add, ALU.mult)

        reciprocal(0, POS, count_banks[0][POS])
        absolute(1)
        reciprocal(0, NEG, count_banks[0][NEG])
        finish(0)
        for side in (POS, NEG):
            reciprocal(1, side, count_banks[1][side])
        one_sidedness(1)
        finish(1)
